import numpy as np
import ml_dtypes


def mxq(x, axis, fmt="e4m3"):
    dtype, down = {"e4m3": (ml_dtypes.float8_e4m3fn, 7), "e5m2": (ml_dtypes.float8_e5m2, 14)}[fmt]
    v = np.moveaxis(np.asarray(x, np.float32).astype(ml_dtypes.bfloat16).astype(np.float64), axis, -1)
    blocks = v.reshape(v.shape[:-1] + (-1, 32))
    amax = np.abs(blocks).max(-1, keepdims=True)
    byte = np.maximum(np.where(amax > 0, np.frexp(amax)[1] - 1 + 127, 0) - down, 1)
    scale = np.exp2(byte - 127.0)
    codes = (blocks / scale).astype(np.float32).astype(dtype).astype(np.float64)
    return np.moveaxis((codes * scale).reshape(v.shape), -1, axis)


WIDE = False


def mx_kscale(k):
    if not WIDE:
        return np.ones(k)
    levels = np.array([10, -10, 5, -5, 0])
    if k % 512:
        return np.exp2(np.random.permutation(np.resize(levels, k // 32))).repeat(32)
    a = np.empty((k // 512, 16))
    for p in range(k // 512):
        a[p, :8] = np.random.permutation(np.resize(levels, 8))
        for g in range(8):
            far = levels[np.abs(levels - a[p, g]) >= 10]
            a[p, g + 8] = far[np.random.randint(len(far))]
    return np.exp2(a.ravel()).repeat(32)


def f64(x):
    return np.asarray(x).astype(np.float64)


def striped(idx):
    return np.tile(idx.reshape(-1, 16).T, (8, 1)).astype(np.uint16)


def unstriped(offs):
    return offs[:16].T.reshape(-1).astype(np.int64)


def striped8(idx):
    return np.concatenate([x.reshape(-1, 16).T for x in idx]).astype(np.uint16)


def runs(offs, k):
    lists = np.stack([offs[16 * r : 16 * r + 16].T.reshape(-1) for r in range(8)]).astype(np.int64)
    return lists[np.arange(k) % 512 // 64]


def pack_weight(w):
    k, n = w.shape
    w = f64(np.asarray(w, np.float32).astype(ml_dtypes.bfloat16)).reshape(k // 32, 32, n)
    amax = np.abs(w).max(1)
    byte = np.clip(np.where(amax > 0, np.frexp(amax)[1] - 1 + 127 - 7, 1), 1, 254)
    scaled = (w * np.exp2(127.0 - byte)[:, None, :]).reshape(k, n).astype(np.float32)
    words = np.ascontiguousarray(scaled.reshape(k // 512, 128, 4, n).transpose(0, 1, 3, 2)).astype(ml_dtypes.float8_e4m3fn).view(np.uint8)
    return words, np.ascontiguousarray(byte.astype(np.uint8).reshape(k // 512, 16, n))


def unpack_weight(words, scales):
    g, p, n, _ = words.shape
    vals = np.ascontiguousarray(words).view(ml_dtypes.float8_e4m3fn).astype(np.float64) * np.repeat(np.exp2(scales.astype(np.float64) - 127.0), 8, axis=1)[..., None]
    return vals.transpose(0, 1, 3, 2).reshape(g * 512, n)


K, T, S, G, H = 512, 2048, 512, 2048, 512


def setup_inputs():
    n = np.random.standard_normal
    s = mx_kscale(K)[:, None]
    packed_xT = pack_weight(n((K, T)) * s)
    packed_dT = pack_weight(n((K, G)) / s)
    return {
        "x_words": packed_xT[0],
        "x_scales": packed_xT[1],
        "d_words": packed_dT[0],
        "d_scales": packed_dT[1],
        "gs": (np.random.uniform(0.5, 1.5, (K, 1)) * s).astype(np.float32),
        "offs": striped(np.random.permutation(T)[:S]),
        "k1": striped8(np.random.randint(0, G, (8, H))),
        "n1": striped8(np.stack([np.random.permutation(S) for _ in range(8)])),
        "n2": striped8(np.stack([np.random.permutation(S) for _ in range(8)])),
        "k2": striped8(np.random.randint(0, G, (8, H))),
    }


def reference(x_words, x_scales, d_words, d_scales, gs, offs, k1, n1, n2, k2):
    d_k2 = unpack_weight(d_words, d_scales)[np.arange(K)[:, None], runs(k2, K)]
    d_k1 = unpack_weight(d_words, d_scales)[np.arange(K)[:, None], runs(k1, K)]
    xq = unpack_weight(x_words, x_scales)[:, unstriped(offs)]
    h = 0.0625 * (d_k1.T @ xq)
    a = h[np.arange(H)[:, None], runs(n1, H)]
    b = h[np.arange(H)[:, None], runs(n2, H)]
    z = f64(gs) * (np.maximum(np.minimum(h, a), np.minimum(np.maximum(h, a), b)))
    return 0.0625 * ((d_k2.T @ mxq(z, 0, "e4m3")))

@@ -1,0 +1,162 @@
+from contextlib import ExitStack
+
+import concourse.mybir as mybir
+
+K, T, S, G, H = 512, 2048, 512, 2048, 512
+FLOPS = 2 * 2 * 512 * 512 * 512
+
+F32 = mybir.dt.float32
+BF16 = mybir.dt.bfloat16
+I32 = mybir.dt.int32
+U32 = mybir.dt.uint32
+U16 = mybir.dt.uint16
+U8 = mybir.dt.uint8
+FP8X4 = mybir.dt.float8_e4m3fn_x4
+COPY = mybir.ActivationFunctionType.Copy
+MIN = mybir.AluOpType.min
+MAX = mybir.AluOpType.max
+MULT = mybir.AluOpType.mult
+
+P = 128
+PACK = 4
+PIECE = 256
+
+
+def tile_picked_pqmed_none_p_kernel(
+    tc, x_words, x_scales, d_words, d_scales, gs, offs, k1, n1, n2, k2, out
+):
+    nc = tc.nc
+    with ExitStack() as ctx:
+        lists = ctx.enter_context(tc.tile_pool(name="lists", bufs=1))
+        keep = ctx.enter_context(tc.tile_pool(name="keep", bufs=1))
+        psum = ctx.enter_context(tc.psum_pool(name="psum", bufs=1))
+
+        def load_list(src, name):
+            tile = lists.tile([P, S // 16], U16, name=name)
+            nc.sync.dma_start(tile[:], src)
+            return tile
+
+        d_sc = keep.tile([P, G], U8, name="d_sc", align_bytes=64)
+        x_sc = keep.tile([P, T], U8, name="x_sc", align_bytes=64)
+        nc.vector.memset(x_sc[:].bitcast(I32), 0)
+        w2_sc = keep.tile([P, H], U8, name="w2_sc", align_bytes=64)
+        nc.vector.memset(w2_sc[:].bitcast(I32), 0)
+
+        k1_sb = load_list(k1, "k1_sb")
+        nc.sync.dma_start(d_sc[:].bitcast(I32), d_scales[0].bitcast(I32).unsqueeze(1).to_broadcast([16, 8, G // 4]))
+        k2_sb = load_list(k2, "k2_sb")
+        offs_sb = load_list(offs, "offs_sb")
+        n1_sb = load_list(n1, "n1_sb")
+        n2_sb = load_list(n2, "n2_sb")
+        gs_sb = keep.tile([P, PACK], F32, name="gs_sb")
+        nc.sync.dma_start(gs_sb[:], gs.rearrange("(p t) o -> p (t o)", t=PACK))
+        d_w = keep.tile([P, G], U32, name="d_w", align_bytes=64)
+        nc.sync.dma_start(d_w[:].bitcast(I32), d_words[0].rearrange("p n t -> p (n t)").bitcast(I32))
+        x_w = keep.tile([P, T], U32, name="x_w", tag="x_w", align_bytes=64)
+        nc.sync.dma_start(x_w[:].bitcast(I32), x_words[0].rearrange("p n t -> p (n t)").bitcast(I32))
+        x_rows = x_scales[0].bitcast(I32)
+        for q in range(4):
+            nc.scalar.dma_start(x_sc[32 * q : 32 * q + 4, :].bitcast(I32), x_rows[4 * q : 4 * q + 4, :])
+        gs16 = keep.tile([P, PACK], F32, name="gs16")
+        nc.scalar.activation(gs16[:], gs_sb[:], COPY, scale=0.0625)
+
+        w1_sc_g = keep.tile([P, H], U8, name="w1_sc_g", align_bytes=64)
+        nc.vector.tensor_copy(w1_sc_g[:], d_sc[:].indirect(k1_sb[:]))
+        w1_sc = keep.tile([P, H], U8, name="w1_sc", align_bytes=64)
+        nc.vector.tensor_copy(
+            w1_sc[:].rearrange("p (t c i) -> p c t i", t=PACK, i=16),
+            w1_sc_g[:].rearrange("p (c i t) -> p c t i", t=PACK, i=16),
+        )
+        for row in range(1, 4):
+            nc.scalar.dma_start(w1_sc[row:P:32, :].bitcast(I32), w1_sc[8 * row : P : 32, :].bitcast(I32))
+
+        w2_sc_g = keep.tile([P, H], U8, name="w2_sc_g", align_bytes=64)
+        nc.vector.tensor_copy(w2_sc_g[:], d_sc[:].indirect(k2_sb[:]))
+        for row in range(4):
+            nc.sync.dma_start(w2_sc[row:P:32, :].bitcast(I32), w2_sc_g[8 * row : P : 32, :].bitcast(I32))
+
+        w1_g = keep.tile([P, H], U32, name="w1_g", align_bytes=64)
+        nc.vector.tensor_copy(w1_g[:], d_w[:].indirect(k1_sb[:]))
+        w1 = keep.tile([P, H], U32, name="w1", align_bytes=64)
+        nc.vector.tensor_copy(
+            w1[:].rearrange("p (t c i) -> p c t i", t=PACK, i=4),
+            w1_g[:].rearrange("p (c i t) -> p c t i", t=PACK, i=4),
+        )
+        xq_sc = keep.tile([P, S], U8, name="xq_sc", align_bytes=64)
+        nc.vector.tensor_copy(xq_sc[:], x_sc[:].indirect(offs_sb[:]))
+        xq = keep.tile([P, S], U32, name="xq", align_bytes=64)
+        nc.vector.tensor_copy(xq[:], x_w[:].indirect(offs_sb[:]))
+        w2 = keep.tile([P, H], U32, name="w2", tag="x_w", align_bytes=64)
+        nc.vector.tensor_copy(w2[:], d_w[:].indirect(k2_sb[:]))
+
+        pieces = S // PIECE
+        h = []
+        for t in range(PACK):
+            cols = slice(t * P, (t + 1) * P)
+            acc = psum.tile([P, S], F32, name="acc%d" % t)
+            nc.tensor.matmul_mx(
+                out=acc[:], lhsT=w1[:, cols].bitcast(FP8X4), lhsT_scale=w1_sc[:, cols],
+                rhs=xq[:].bitcast(FP8X4), rhs_scale=xq_sc[:], start=True, stop=True,
+            )
+            h_t = keep.tile([P, S], F32, name="h%d" % t, align_bytes=64)
+            nc.scalar.activation(h_t[:], acc[:], COPY, scale=gs16[:, t : t + 1])
+            h.append(h_t)
+
+        hb = keep.tile([P, pieces, PACK, PIECE], BF16, name="hb", align_bytes=64)
+        for t in range(PACK):
+            nc.scalar.copy(hb[:, :, t, :], h[t][:].rearrange("p (c n) -> p c n", c=pieces))
+
+        def interleave(engine_copy, zi, z, c0, c1):
+            dst = zi[:, c0 * PACK : c1 * PACK].rearrange("p (c i t) -> p c t i", i=4, t=PACK)
+            engine_copy(dst, z[:, :, c0:c1].rearrange("p t (c i) -> p c t i", i=4))
+
+        for c in range(pieces):
+            last = c == pieces - 1
+            cols = slice(c * PIECE, (c + 1) * PIECE)
+            ent = slice(c * PIECE // 16, (c + 1) * PIECE // 16)
+            a = keep.tile([P, PACK, PIECE], BF16, name="a", tag="a", align_bytes=64)
+            b = keep.tile([P, PACK, PIECE], BF16, name="b", tag="bz%d" % c, align_bytes=64)
+            for t in range(PACK):
+                nc.vector.tensor_copy(a[:, t, :], h[t][:].indirect(n1_sb[:, ent]))
+            hi = keep.tile([P, PACK, PIECE], BF16, name="hi%d" % c, align_bytes=64)
+            lo = keep.tile([P, PACK, PIECE], BF16, name="lo%d" % c, align_bytes=64)
+            mid = keep.tile([P, PACK, PIECE], BF16, name="mid%d" % c, align_bytes=64)
+            z = keep.tile([P, PACK, PIECE], BF16, name="z%d" % c, align_bytes=64)
+            for t in range(PACK):
+                nc.vector.tensor_copy(b[:, t, :], h[t][:].indirect(n2_sb[:, ent]))
+            nc.vector.tensor_tensor(hi[:], hb[:, c], a[:], MAX)
+            nc.vector.tensor_tensor(lo[:], hb[:, c], a[:], MIN)
+            nc.vector.tensor_tensor(mid[:], hi[:], b[:], MIN)
+            zq = keep.tile([P, PIECE], U32, name="zq%d" % c, align_bytes=64)
+            zq_sc = keep.tile([P, PIECE], U8, name="zq_sc%d" % c, align_bytes=64)
+            if not last:
+                nc.vector.tensor_tensor(z[:], lo[:], mid[:], MAX)
+                zi = keep.tile([P, PIECE * PACK], BF16, name="zi", tag="bz%d" % (c + 1), align_bytes=64)
+                interleave(nc.scalar.copy, zi, z, 0, PIECE)
+                nc.vector.quantize_mx(out=zq[:].bitcast(FP8X4), scales=zq_sc[:], in_=zi[:])
+            else:
+                half = PIECE // 2
+                zi = keep.tile([P, PIECE * PACK], BF16, name="zi_last", align_bytes=64)
+                for c0, engine_copy in ((0, nc.scalar.copy), (half, nc.vector.tensor_copy)):
+                    part = slice(c0, c0 + half)
+                    nc.vector.tensor_tensor(z[:, :, part], lo[:, :, part], mid[:, :, part], MAX)
+                    interleave(engine_copy, zi, z, c0, c0 + half)
+                for c0 in (half, 0):
+                    part = slice(c0, c0 + half)
+                    nc.vector.quantize_mx(
+                        out=zq[:, part].bitcast(FP8X4), scales=zq_sc[:, part],
+                        in_=zi[:, c0 * PACK : (c0 + half) * PACK],
+                    )
+            for m in range(4):
+                rows = slice(m * P, (m + 1) * P)
+                acc2 = psum.tile([P, PIECE], F32, name="out%d" % m)
+                nc.tensor.matmul_mx(
+                    out=acc2[:], lhsT=w2[:, rows].bitcast(FP8X4), lhsT_scale=w2_sc[:, rows],
+                    rhs=zq[:].bitcast(FP8X4), rhs_scale=zq_sc[:], start=True, stop=True,
+                )
+                res = keep.tile([P, PIECE], F32, name="res%d_%d" % (c, m))
+                if last and m % 2 == 1:
+                    nc.vector.tensor_scalar(res[:], acc2[:], 0.0625, None, MULT)
+                else:
+                    nc.scalar.activation(res[:], acc2[:], COPY, scale=0.0625)
+                nc.sync.dma_start(out[rows, cols], res[:])

@@ -38,7 +38,6 @@ def tile_picked_pqmed_none_p_kernel(
 
         d_sc = keep.tile([P, G], U8, name="d_sc", align_bytes=64)
         x_sc = keep.tile([P, T], U8, name="x_sc", align_bytes=64)
-        nc.vector.memset(x_sc[:].bitcast(I32), 0)
         w2_sc = keep.tile([P, H], U8, name="w2_sc", align_bytes=64)
         nc.vector.memset(w2_sc[:].bitcast(I32), 0)
 
@@ -46,17 +45,20 @@ def tile_picked_pqmed_none_p_kernel(
         nc.sync.dma_start(d_sc[:].bitcast(I32), d_scales[0].bitcast(I32).unsqueeze(1).to_broadcast([16, 8, G // 4]))
         k2_sb = load_list(k2, "k2_sb")
         offs_sb = load_list(offs, "offs_sb")
-        n1_sb = load_list(n1, "n1_sb")
-        n2_sb = load_list(n2, "n2_sb")
-        gs_sb = keep.tile([P, PACK], F32, name="gs_sb")
-        nc.sync.dma_start(gs_sb[:], gs.rearrange("(p t) o -> p (t o)", t=PACK))
+        x_rows = x_scales[0].bitcast(I32)
+        for q in range(4):
+            nc.sync.dma_start(
+                x_sc[32 * q : 32 * q + 32, :].bitcast(I32),
+                x_rows[4 * q : 4 * q + 4, :].unsqueeze(0).to_broadcast([8, 4, T // 4]),
+            )
         d_w = keep.tile([P, G], U32, name="d_w", align_bytes=64)
         nc.sync.dma_start(d_w[:].bitcast(I32), d_words[0].rearrange("p n t -> p (n t)").bitcast(I32))
         x_w = keep.tile([P, T], U32, name="x_w", tag="x_w", align_bytes=64)
         nc.sync.dma_start(x_w[:].bitcast(I32), x_words[0].rearrange("p n t -> p (n t)").bitcast(I32))
-        x_rows = x_scales[0].bitcast(I32)
-        for q in range(4):
-            nc.scalar.dma_start(x_sc[32 * q : 32 * q + 4, :].bitcast(I32), x_rows[4 * q : 4 * q + 4, :])
+        n1_sb = load_list(n1, "n1_sb")
+        n2_sb = load_list(n2, "n2_sb")
+        gs_sb = keep.tile([P, PACK], F32, name="gs_sb")
+        nc.sync.dma_start(gs_sb[:], gs.rearrange("(p t) o -> p (t o)", t=PACK))
         gs16 = keep.tile([P, PACK], F32, name="gs16")
         nc.scalar.activation(gs16[:], gs_sb[:], COPY, scale=0.0625)
 
@@ -85,7 +87,11 @@ def tile_picked_pqmed_none_p_kernel(
         xq_sc = keep.tile([P, S], U8, name="xq_sc", align_bytes=64)
         nc.vector.tensor_copy(xq_sc[:], x_sc[:].indirect(offs_sb[:]))
         xq = keep.tile([P, S], U32, name="xq", align_bytes=64)
-        nc.vector.tensor_copy(xq[:], x_w[:].indirect(offs_sb[:]))
+        for c in range(S // PIECE):
+            nc.vector.tensor_copy(
+                xq[:, c * PIECE : (c + 1) * PIECE],
+                x_w[:].indirect(offs_sb[:, c * PIECE // 16 : (c + 1) * PIECE // 16]),
+            )
         w2 = keep.tile([P, H], U32, name="w2", tag="x_w", align_bytes=64)
         nc.vector.tensor_copy(w2[:], d_w[:].indirect(k2_sb[:]))
 
@@ -93,63 +99,66 @@ def tile_picked_pqmed_none_p_kernel(
         h = []
         for t in range(PACK):
             cols = slice(t * P, (t + 1) * P)
-            acc = psum.tile([P, S], F32, name="acc%d" % t)
-            nc.tensor.matmul_mx(
-                out=acc[:], lhsT=w1[:, cols].bitcast(FP8X4), lhsT_scale=w1_sc[:, cols],
-                rhs=xq[:].bitcast(FP8X4), rhs_scale=xq_sc[:], start=True, stop=True,
-            )
-            h_t = keep.tile([P, S], F32, name="h%d" % t, align_bytes=64)
-            nc.scalar.activation(h_t[:], acc[:], COPY, scale=gs16[:, t : t + 1])
+            h_t = keep.tile([P, 2 * S if t < 2 else S], F32, name="h%d" % t, align_bytes=64)
+            if t < 2:
+                nc.vector.memset(h_t[:, S:], 0.0)
+            width = PIECE if t == 0 else S
+            for c0 in range(0, S, width):
+                part = slice(c0, c0 + width)
+                acc = psum.tile([P, width], F32, name="acc", tag="bank%d" % (t if c0 == 0 else PACK))
+                nc.tensor.matmul_mx(
+                    out=acc[:], lhsT=w1[:, cols].bitcast(FP8X4), lhsT_scale=w1_sc[:, cols],
+                    rhs=xq[:, part].bitcast(FP8X4), rhs_scale=xq_sc[:, part], start=True, stop=True,
+                )
+                nc.scalar.activation(h_t[:, part], acc[:], COPY, scale=gs16[:, t : t + 1])
             h.append(h_t)
 
-        hb = keep.tile([P, pieces, PACK, PIECE], BF16, name="hb", align_bytes=64)
-        for t in range(PACK):
-            nc.scalar.copy(hb[:, :, t, :], h[t][:].rearrange("p (c n) -> p c n", c=pieces))
+        hb = []
+        for u in range(2):
+            hb_u = keep.tile([P, 2, S], BF16, name="hb%d" % u, align_bytes=64)
+            for e in range(2):
+                nc.scalar.copy(hb_u[:, e, :], h[2 * u + e][:, :S])
+            hb.append(hb_u)
 
-        def interleave(engine_copy, zi, z, c0, c1):
-            dst = zi[:, c0 * PACK : c1 * PACK].rearrange("p (c i t) -> p c t i", i=4, t=PACK)
-            engine_copy(dst, z[:, :, c0:c1].rearrange("p t (c i) -> p c t i", i=4))
+        def median(u, c0, width, parts, a_tag, b_tag):
+            ent = slice(c0 // 16, (c0 + width) // 16)
+            key = "%d_%d" % (u, c0)
+            a = keep.tile([P, 2, width], BF16, name="a", tag=a_tag, align_bytes=64)
+            b = keep.tile([P, 2, width], BF16, name="b", tag=b_tag, align_bytes=64)
+            hi = keep.tile([P, 2, width], BF16, name="hi", tag="hi" + key, align_bytes=64)
+            lo = keep.tile([P, 2, width], BF16, name="lo" + key, align_bytes=64)
+            mid = keep.tile([P, 2, width], BF16, name="mid" + key, align_bytes=64)
+            z = keep.tile([P, 2, width], BF16, name="z" + key, align_bytes=64)
+            own = hb[u][:, :, c0 : c0 + width]
+            for e in range(2):
+                nc.vector.tensor_copy(a[:, e, :], h[2 * u + e][:].indirect(n1_sb[:, ent]))
+            nc.vector.tensor_copy(b[:, 0, :], h[2 * u][:].indirect(n2_sb[:, ent]))
+            nc.vector.tensor_tensor(hi[:], own, a[:], MAX)
+            nc.vector.tensor_tensor(lo[:], own, a[:], MIN)
+            nc.vector.tensor_copy(b[:, 1, :], h[2 * u + 1][:].indirect(n2_sb[:, ent]))
+            for part in parts:
+                nc.vector.tensor_tensor(mid[:, :, part], hi[:, :, part], b[:, :, part], MIN)
+            for part in parts:
+                nc.vector.tensor_tensor(z[:, :, part], lo[:, :, part], mid[:, :, part], MAX)
+            return z
 
-        for c in range(pieces):
+        def interleave(copy, zi, part, u, z):
+            dst = zi[:].rearrange("p (n t) -> p n t", t=PACK)[:, part, 2 * u : 2 * u + 2]
+            copy(dst.rearrange("p (c i) e -> p c e i", i=4), z.rearrange("p e (c i) -> p c e i", i=4))
+
+        def second_product(c, zi, parts):
             last = c == pieces - 1
             cols = slice(c * PIECE, (c + 1) * PIECE)
-            ent = slice(c * PIECE // 16, (c + 1) * PIECE // 16)
-            a = keep.tile([P, PACK, PIECE], BF16, name="a", tag="a", align_bytes=64)
-            b = keep.tile([P, PACK, PIECE], BF16, name="b", tag="bz%d" % c, align_bytes=64)
-            for t in range(PACK):
-                nc.vector.tensor_copy(a[:, t, :], h[t][:].indirect(n1_sb[:, ent]))
-            hi = keep.tile([P, PACK, PIECE], BF16, name="hi%d" % c, align_bytes=64)
-            lo = keep.tile([P, PACK, PIECE], BF16, name="lo%d" % c, align_bytes=64)
-            mid = keep.tile([P, PACK, PIECE], BF16, name="mid%d" % c, align_bytes=64)
-            z = keep.tile([P, PACK, PIECE], BF16, name="z%d" % c, align_bytes=64)
-            for t in range(PACK):
-                nc.vector.tensor_copy(b[:, t, :], h[t][:].indirect(n2_sb[:, ent]))
-            nc.vector.tensor_tensor(hi[:], hb[:, c], a[:], MAX)
-            nc.vector.tensor_tensor(lo[:], hb[:, c], a[:], MIN)
-            nc.vector.tensor_tensor(mid[:], hi[:], b[:], MIN)
             zq = keep.tile([P, PIECE], U32, name="zq%d" % c, align_bytes=64)
             zq_sc = keep.tile([P, PIECE], U8, name="zq_sc%d" % c, align_bytes=64)
-            if not last:
-                nc.vector.tensor_tensor(z[:], lo[:], mid[:], MAX)
-                zi = keep.tile([P, PIECE * PACK], BF16, name="zi", tag="bz%d" % (c + 1), align_bytes=64)
-                interleave(nc.scalar.copy, zi, z, 0, PIECE)
-                nc.vector.quantize_mx(out=zq[:].bitcast(FP8X4), scales=zq_sc[:], in_=zi[:])
-            else:
-                half = PIECE // 2
-                zi = keep.tile([P, PIECE * PACK], BF16, name="zi_last", align_bytes=64)
-                for c0, engine_copy in ((0, nc.scalar.copy), (half, nc.vector.tensor_copy)):
-                    part = slice(c0, c0 + half)
-                    nc.vector.tensor_tensor(z[:, :, part], lo[:, :, part], mid[:, :, part], MAX)
-                    interleave(engine_copy, zi, z, c0, c0 + half)
-                for c0 in (half, 0):
-                    part = slice(c0, c0 + half)
-                    nc.vector.quantize_mx(
-                        out=zq[:, part].bitcast(FP8X4), scales=zq_sc[:, part],
-                        in_=zi[:, c0 * PACK : (c0 + half) * PACK],
-                    )
+            for part in parts:
+                nc.vector.quantize_mx(
+                    out=zq[:, part].bitcast(FP8X4), scales=zq_sc[:, part],
+                    in_=zi[:, part.start * PACK : part.stop * PACK],
+                )
             for m in range(4):
                 rows = slice(m * P, (m + 1) * P)
-                acc2 = psum.tile([P, PIECE], F32, name="out%d" % m)
+                acc2 = psum.tile([P, PIECE], F32, name="acc2", tag="bank%d" % (PACK * (1 - c) + m))
                 nc.tensor.matmul_mx(
                     out=acc2[:], lhsT=w2[:, rows].bitcast(FP8X4), lhsT_scale=w2_sc[:, rows],
                     rhs=zq[:].bitcast(FP8X4), rhs_scale=zq_sc[:], start=True, stop=True,
@@ -160,3 +169,17 @@ def tile_picked_pqmed_none_p_kernel(
                 else:
                     nc.scalar.activation(res[:], acc2[:], COPY, scale=0.0625)
                 nc.sync.dma_start(out[rows, cols], res[:])
+
+        whole = slice(0, PIECE)
+        halves = [slice(0, PIECE // 2), slice(PIECE // 2, PIECE)]
+        zi = [keep.tile([P, PIECE * PACK], BF16, name="zi", tag="zi%d" % c, align_bytes=64) for c in range(pieces)]
+        z = median(0, 0, S, [slice(0, S)], "a0", "b0")
+        for c in range(pieces):
+            interleave(nc.scalar.copy, zi[c], whole, 0, z[:, :, c * PIECE : (c + 1) * PIECE])
+        z = median(1, 0, PIECE, [whole], "a1", "b1")
+        interleave(nc.scalar.copy, zi[0], whole, 1, z[:])
+        second_product(0, zi[0], [whole])
+        z = median(1, PIECE, PIECE, halves, "hi1_0", "zi0")
+        for part in halves:
+            interleave(nc.vector.tensor_copy, zi[1], part, 1, z[:, :, part])
+        second_product(1, zi[1], halves)

from contextlib import ExitStack

import concourse.mybir as mybir

K, T, S, G, H = 512, 2048, 512, 2048, 512
FLOPS = 2 * 2 * 512 * 512 * 512

F32 = mybir.dt.float32
BF16 = mybir.dt.bfloat16
I32 = mybir.dt.int32
U32 = mybir.dt.uint32
U16 = mybir.dt.uint16
U8 = mybir.dt.uint8
FP8X4 = mybir.dt.float8_e4m3fn_x4
COPY = mybir.ActivationFunctionType.Copy
MIN = mybir.AluOpType.min
MAX = mybir.AluOpType.max
MULT = mybir.AluOpType.mult

P = 128
PACK = 4
PIECE = 256


def tile_picked_pqmed_none_p_kernel(
    tc, x_words, x_scales, d_words, d_scales, gs, offs, k1, n1, n2, k2, out
):
    nc = tc.nc
    with ExitStack() as ctx:
        lists = ctx.enter_context(tc.tile_pool(name="lists", bufs=1))
        keep = ctx.enter_context(tc.tile_pool(name="keep", bufs=1))
        psum = ctx.enter_context(tc.psum_pool(name="psum", bufs=1))

        def load_list(src, name):
            tile = lists.tile([P, S // 16], U16, name=name)
            nc.sync.dma_start(tile[:], src)
            return tile

        d_sc = keep.tile([P, G], U8, name="d_sc", align_bytes=64)
        x_sc = keep.tile([P, T], U8, name="x_sc", align_bytes=64)
        w2_sc = keep.tile([P, H], U8, name="w2_sc", align_bytes=64)
        nc.vector.memset(w2_sc[:].bitcast(I32), 0)

        k1_sb = load_list(k1, "k1_sb")
        nc.sync.dma_start(d_sc[:].bitcast(I32), d_scales[0].bitcast(I32).unsqueeze(1).to_broadcast([16, 8, G // 4]))
        k2_sb = load_list(k2, "k2_sb")
        offs_sb = load_list(offs, "offs_sb")
        x_rows = x_scales[0].bitcast(I32)
        for q in range(4):
            nc.sync.dma_start(
                x_sc[32 * q : 32 * q + 32, :].bitcast(I32),
                x_rows[4 * q : 4 * q + 4, :].unsqueeze(0).to_broadcast([8, 4, T // 4]),
            )
        d_w = keep.tile([P, G], U32, name="d_w", align_bytes=64)
        nc.sync.dma_start(d_w[:].bitcast(I32), d_words[0].rearrange("p n t -> p (n t)").bitcast(I32))
        x_w = keep.tile([P, T], U32, name="x_w", tag="x_w", align_bytes=64)
        nc.sync.dma_start(x_w[:].bitcast(I32), x_words[0].rearrange("p n t -> p (n t)").bitcast(I32))
        n1_sb = load_list(n1, "n1_sb")
        n2_sb = load_list(n2, "n2_sb")
        gs_sb = keep.tile([P, PACK], F32, name="gs_sb")
        nc.sync.dma_start(gs_sb[:], gs.rearrange("(p t) o -> p (t o)", t=PACK))
        gs16 = keep.tile([P, PACK], F32, name="gs16")
        nc.scalar.activation(gs16[:], gs_sb[:], COPY, scale=0.0625)

        w1_sc_g = keep.tile([P, H], U8, name="w1_sc_g", align_bytes=64)
        nc.vector.tensor_copy(w1_sc_g[:], d_sc[:].indirect(k1_sb[:]))
        w1_sc = keep.tile([P, H], U8, name="w1_sc", align_bytes=64)
        nc.vector.tensor_copy(
            w1_sc[:].rearrange("p (t c i) -> p c t i", t=PACK, i=16),
            w1_sc_g[:].rearrange("p (c i t) -> p c t i", t=PACK, i=16),
        )
        for row in range(1, 4):
            nc.scalar.dma_start(w1_sc[row:P:32, :].bitcast(I32), w1_sc[8 * row : P : 32, :].bitcast(I32))

        w2_sc_g = keep.tile([P, H], U8, name="w2_sc_g", align_bytes=64)
        nc.vector.tensor_copy(w2_sc_g[:], d_sc[:].indirect(k2_sb[:]))
        for row in range(4):
            nc.sync.dma_start(w2_sc[row:P:32, :].bitcast(I32), w2_sc_g[8 * row : P : 32, :].bitcast(I32))

        w1_g = keep.tile([P, H], U32, name="w1_g", align_bytes=64)
        nc.vector.tensor_copy(w1_g[:], d_w[:].indirect(k1_sb[:]))
        w1 = keep.tile([P, H], U32, name="w1", align_bytes=64)
        nc.vector.tensor_copy(
            w1[:].rearrange("p (t c i) -> p c t i", t=PACK, i=4),
            w1_g[:].rearrange("p (c i t) -> p c t i", t=PACK, i=4),
        )
        xq_sc = keep.tile([P, S], U8, name="xq_sc", align_bytes=64)
        nc.vector.tensor_copy(xq_sc[:], x_sc[:].indirect(offs_sb[:]))
        xq = keep.tile([P, S], U32, name="xq", align_bytes=64)
        for c in range(S // PIECE):
            nc.vector.tensor_copy(
                xq[:, c * PIECE : (c + 1) * PIECE],
                x_w[:].indirect(offs_sb[:, c * PIECE // 16 : (c + 1) * PIECE // 16]),
            )
        w2 = keep.tile([P, H], U32, name="w2", tag="x_w", align_bytes=64)
        nc.vector.tensor_copy(w2[:], d_w[:].indirect(k2_sb[:]))

        pieces = S // PIECE
        h = []
        for t in range(PACK):
            cols = slice(t * P, (t + 1) * P)
            h_t = keep.tile([P, 2 * S if t < 2 else S], F32, name="h%d" % t, align_bytes=64)
            if t < 2:
                nc.vector.memset(h_t[:, S:], 0.0)
            width = PIECE if t == 0 else S
            for c0 in range(0, S, width):
                part = slice(c0, c0 + width)
                acc = psum.tile([P, width], F32, name="acc", tag="bank%d" % (t if c0 == 0 else PACK))
                nc.tensor.matmul_mx(
                    out=acc[:], lhsT=w1[:, cols].bitcast(FP8X4), lhsT_scale=w1_sc[:, cols],
                    rhs=xq[:, part].bitcast(FP8X4), rhs_scale=xq_sc[:, part], start=True, stop=True,
                )
                nc.scalar.activation(h_t[:, part], acc[:], COPY, scale=gs16[:, t : t + 1])
            h.append(h_t)

        hb = []
        for u in range(2):
            hb_u = keep.tile([P, 2, S], BF16, name="hb%d" % u, align_bytes=64)
            for e in range(2):
                nc.scalar.copy(hb_u[:, e, :], h[2 * u + e][:, :S])
            hb.append(hb_u)

        def median(u, c0, width, parts, a_tag, b_tag):
            ent = slice(c0 // 16, (c0 + width) // 16)
            key = "%d_%d" % (u, c0)
            a = keep.tile([P, 2, width], BF16, name="a", tag=a_tag, align_bytes=64)
            b = keep.tile([P, 2, width], BF16, name="b", tag=b_tag, align_bytes=64)
            hi = keep.tile([P, 2, width], BF16, name="hi", tag="hi" + key, align_bytes=64)
            lo = keep.tile([P, 2, width], BF16, name="lo" + key, align_bytes=64)
            mid = keep.tile([P, 2, width], BF16, name="mid" + key, align_bytes=64)
            z = keep.tile([P, 2, width], BF16, name="z" + key, align_bytes=64)
            own = hb[u][:, :, c0 : c0 + width]
            for e in range(2):
                nc.vector.tensor_copy(a[:, e, :], h[2 * u + e][:].indirect(n1_sb[:, ent]))
            nc.vector.tensor_copy(b[:, 0, :], h[2 * u][:].indirect(n2_sb[:, ent]))
            nc.vector.tensor_tensor(hi[:], own, a[:], MAX)
            nc.vector.tensor_tensor(lo[:], own, a[:], MIN)
            nc.vector.tensor_copy(b[:, 1, :], h[2 * u + 1][:].indirect(n2_sb[:, ent]))
            for part in parts:
                nc.vector.tensor_tensor(mid[:, :, part], hi[:, :, part], b[:, :, part], MIN)
            for part in parts:
                nc.vector.tensor_tensor(z[:, :, part], lo[:, :, part], mid[:, :, part], MAX)
            return z

        def interleave(copy, zi, part, u, z):
            dst = zi[:].rearrange("p (n t) -> p n t", t=PACK)[:, part, 2 * u : 2 * u + 2]
            copy(dst.rearrange("p (c i) e -> p c e i", i=4), z.rearrange("p e (c i) -> p c e i", i=4))

        def second_product(c, zi, parts):
            last = c == pieces - 1
            cols = slice(c * PIECE, (c + 1) * PIECE)
            zq = keep.tile([P, PIECE], U32, name="zq%d" % c, align_bytes=64)
            zq_sc = keep.tile([P, PIECE], U8, name="zq_sc%d" % c, align_bytes=64)
            for part in parts:
                nc.vector.quantize_mx(
                    out=zq[:, part].bitcast(FP8X4), scales=zq_sc[:, part],
                    in_=zi[:, part.start * PACK : part.stop * PACK],
                )
            for m in range(4):
                rows = slice(m * P, (m + 1) * P)
                acc2 = psum.tile([P, PIECE], F32, name="acc2", tag="bank%d" % (PACK * (1 - c) + m))
                nc.tensor.matmul_mx(
                    out=acc2[:], lhsT=w2[:, rows].bitcast(FP8X4), lhsT_scale=w2_sc[:, rows],
                    rhs=zq[:].bitcast(FP8X4), rhs_scale=zq_sc[:], start=True, stop=True,
                )
                res = keep.tile([P, PIECE], F32, name="res%d_%d" % (c, m))
                if last and m % 2 == 1:
                    nc.vector.tensor_scalar(res[:], acc2[:], 0.0625, None, MULT)
                else:
                    nc.scalar.activation(res[:], acc2[:], COPY, scale=0.0625)
                nc.sync.dma_start(out[rows, cols], res[:])

        whole = slice(0, PIECE)
        halves = [slice(0, PIECE // 2), slice(PIECE // 2, PIECE)]
        zi = [keep.tile([P, PIECE * PACK], BF16, name="zi", tag="zi%d" % c, align_bytes=64) for c in range(pieces)]
        z = median(0, 0, S, [slice(0, S)], "a0", "b0")
        for c in range(pieces):
            interleave(nc.scalar.copy, zi[c], whole, 0, z[:, :, c * PIECE : (c + 1) * PIECE])
        z = median(1, 0, PIECE, [whole], "a1", "b1")
        interleave(nc.scalar.copy, zi[0], whole, 1, z[:])
        second_product(0, zi[0], [whole])
        z = median(1, PIECE, PIECE, halves, "hi1_0", "zi0")
        for part in halves:
            interleave(nc.vector.tensor_copy, zi[1], part, 1, z[:, :, part])
        second_product(1, zi[1], halves)
